import numpy as np
import ml_dtypes


def mxq(x, axis, fmt="e4m3"):
    dtype, down = {"e4m3": (ml_dtypes.float8_e4m3fn, 7), "e5m2": (ml_dtypes.float8_e5m2, 14)}[fmt]
    v = np.moveaxis(np.asarray(x, np.float32).astype(ml_dtypes.bfloat16).astype(np.float64), axis, -1)
    blocks = v.reshape(v.shape[:-1] + (-1, 32))
    amax = np.abs(blocks).max(-1, keepdims=True)
    byte = np.maximum(np.where(amax > 0, np.frexp(amax)[1] - 1 + 127, 0) - down, 1)
    scale = np.exp2(byte - 127.0)
    codes = (blocks / scale).astype(np.float32).astype(dtype).astype(np.float64)
    return np.moveaxis((codes * scale).reshape(v.shape), -1, axis)


WIDE = False


def mx_kscale(k):
    if not WIDE:
        return np.ones(k)
    levels = np.array([10, -10, 5, -5, 0])
    if k % 512:
        return np.exp2(np.random.permutation(np.resize(levels, k // 32))).repeat(32)
    a = np.empty((k // 512, 16))
    for p in range(k // 512):
        a[p, :8] = np.random.permutation(np.resize(levels, 8))
        for g in range(8):
            far = levels[np.abs(levels - a[p, g]) >= 10]
            a[p, g + 8] = far[np.random.randint(len(far))]
    return np.exp2(a.ravel()).repeat(32)


def f64(x):
    return np.asarray(x).astype(np.float64)


def striped(idx):
    return np.tile(idx.reshape(-1, 16).T, (8, 1)).astype(np.uint16)


def unstriped(offs):
    return offs[:16].T.reshape(-1).astype(np.int64)


def pack_weight(w):
    k, n = w.shape
    w = f64(np.asarray(w, np.float32).astype(ml_dtypes.bfloat16)).reshape(k // 32, 32, n)
    amax = np.abs(w).max(1)
    byte = np.clip(np.where(amax > 0, np.frexp(amax)[1] - 1 + 127 - 7, 1), 1, 254)
    scaled = (w * np.exp2(127.0 - byte)[:, None, :]).reshape(k, n).astype(np.float32)
    words = np.ascontiguousarray(scaled.reshape(k // 512, 128, 4, n).transpose(0, 1, 3, 2)).astype(ml_dtypes.float8_e4m3fn).view(np.uint8)
    return words, np.ascontiguousarray(byte.astype(np.uint8).reshape(k // 512, 16, n))


def unpack_weight(words, scales):
    g, p, n, _ = words.shape
    vals = np.ascontiguousarray(words).view(ml_dtypes.float8_e4m3fn).astype(np.float64) * np.repeat(np.exp2(scales.astype(np.float64) - 127.0), 8, axis=1)[..., None]
    return vals.transpose(0, 1, 3, 2).reshape(g * 512, n)


K, T, S, N = 512, 1024, 512, 128
P = 2 ** 7


def setup_inputs():
    n = np.random.standard_normal
    s = mx_kscale(K)[:, None]
    packed_xT = pack_weight(n((K, T)) * s)
    return {
        "x_words": packed_xT[0],
        "x_scales": packed_xT[1],
        "w1": (n((K, N)) / np.sqrt(K) / s).astype(np.float32),
        "w2": (n((K, N)) / np.sqrt(K) / s).astype(np.float32),
        "mu": (n((N, S)) * 0.5).astype(np.float32),
        "cap": (np.tile(np.random.uniform(0.8, 1.5, S), (P, 1))).astype(np.float32),
        "rew": (np.tile(n(S), (P, 1))).astype(np.float32),
        "gam": (np.tile(np.random.uniform(0.6, 0.99, S) * (np.random.uniform(size=S) < 0.95), (P, 1))).astype(np.float32),
        "offs": striped(np.random.permutation(T)[:S]),
    }


def reference(x_words, x_scales, w1, w2, mu, cap, rew, gam, offs):
    xq = unpack_weight(x_words, x_scales)[:, unstriped(offs)]
    yl = mxq(f64(w1), 0, "e4m3").T @ xq
    ratio = np.minimum(np.exp(yl - f64(mu)), f64(cap)[:1])
    val = mxq(f64(w2), 0, "e4m3").T @ xq
    dlt = ratio * (f64(rew)[:1] + f64(gam)[:1] * (np.pad(val, ((0, 0), (0, 1)))[:, 1:]) - val)
    gc = f64(gam)[:1] * ratio
    sa = dlt + gc * (np.pad(dlt, ((0, 0), (0, 1)))[:, 1:])
    cc2 = gc * (np.pad(gc, ((0, 0), (0, 1)))[:, 1:])
    vs = val + sa + cc2 * (np.pad(sa, ((0, 0), (0, 2)))[:, 2:])
    return (ratio * (f64(rew)[:1] + f64(gam)[:1] * (np.pad(vs, ((0, 0), (0, 1)))[:, 1:]) - val)) * (-1.0 * yl)

@@ -1,0 +1,133 @@
+from contextlib import ExitStack
+
+import concourse.mybir as mybir
+
+F32 = mybir.dt.float32
+BF16 = mybir.dt.bfloat16
+I32 = mybir.dt.int32
+U32 = mybir.dt.uint32
+U16 = mybir.dt.uint16
+U8 = mybir.dt.uint8
+FP8X4 = mybir.dt.float8_e4m3fn_x4
+ALU = mybir.AluOpType
+ACT = mybir.ActivationFunctionType
+
+P = 128
+K, T, S, M = 512, 1024, 512, 128
+H = S // 2
+PAD = 8
+FLOPS = 2 * 2 * K * M * S
+
+
+def tile_picked_yvtrac_pol_p_kernel(tc, x_words, x_scales, w1, w2, mu, cap, rew, gam, offs, out):
+    nc = tc.nc
+    with ExitStack() as ctx:
+        sb = ctx.enter_context(tc.tile_pool(name="sb", bufs=1))
+        ps = ctx.enter_context(tc.psum_pool(name="ps", bufs=1))
+
+        offsets = sb.tile([P, S // 16], U16, name="offsets")
+        scale_table = sb.tile([P, T], U8, name="scale_table", align_bytes=64)
+        word_table = sb.tile([P, T], I32, name="word_table", align_bytes=64)
+        w1_raw = sb.tile([P, 4, M], F32, name="w1_raw")
+        w2_raw = sb.tile([P, 4, M], F32, name="w2_raw")
+        mu_t = sb.tile([P, S], F32, name="mu_t")
+        cap_t = sb.tile([P, S], F32, name="cap_t")
+        rew_t = sb.tile([P, S], F32, name="rew_t")
+        gam_t = sb.tile([P, S], F32, name="gam_t")
+
+        nc.sync.dma_start(offsets[:], offs)
+        zero = sb.tile([P, 1], F32, name="zero")
+        nc.gpsimd.memset(scale_table[:].bitcast(I32), 0)
+        nc.gpsimd.memset(zero[:], 0.0)
+        for q in range(4):
+            nc.scalar.dma_start(scale_table[32 * q : 32 * q + 4, :].bitcast(I32), x_scales[0, 4 * q : 4 * q + 4, :].bitcast(I32))
+        nc.sync.dma_start(w1_raw[:], w1.rearrange("(p j) m -> p j m", j=4))
+        nc.sync.dma_start(word_table[:], x_words[0].rearrange("p n t -> p (n t)").bitcast(I32))
+        nc.sync.dma_start(w2_raw[:], w2.rearrange("(p j) m -> p j m", j=4))
+        nc.sync.dma_start(mu_t[:], mu)
+        nc.sync.dma_start(cap_t[:], cap)
+        nc.sync.dma_start(gam_t[:], gam)
+        nc.sync.dma_start(rew_t[:], rew)
+
+        ratio = sb.tile([P, S + PAD], F32, name="ratio")
+        boot = sb.tile([P, S], F32, name="boot")
+        td = sb.tile([P, 2, H + PAD], F32, name="td")
+        pair_sum = sb.tile([P, H + PAD], F32, name="pair_sum")
+        pair_link = sb.tile([P, H + PAD], F32, name="pair_link")
+        quad_sum = sb.tile([P, H + PAD], F32, name="quad_sum")
+        nc.vector.memset(boot[:, S - 1 : S], 0.0)
+        nc.vector.memset(td[:, 0, H:], 0.0)
+        nc.vector.memset(pair_sum[:, H:], 0.0)
+        nc.vector.memset(pair_link[:, H:], 0.0)
+        nc.vector.memset(quad_sum[:, H:], 0.0)
+        nc.scalar.activation(ratio[:, S : S + 1], zero[:], ACT.Exp)
+
+        def quantise(w_raw, name):
+            grouped = sb.tile([P, M, 4], BF16, name=name + "_grouped", align_bytes=64)
+            codes = sb.tile([P, M], U32, name=name + "_codes", align_bytes=64)
+            scales = sb.tile([P, M], U8, name=name + "_scales", align_bytes=64)
+            nc.scalar.copy(grouped[:].rearrange("p (c i) t -> p c t i", i=4), w_raw[:].rearrange("p t (c i) -> p c t i", i=4))
+            nc.vector.quantize_mx(out=codes[:].bitcast(FP8X4), scales=scales[:], in_=grouped[:].rearrange("p m t -> p (m t)"))
+            return codes, scales
+
+        x_codes = sb.tile([P, S], U32, name="x_codes", align_bytes=64)
+        x_sc = sb.tile([P, S], U8, name="x_sc", align_bytes=64)
+        nc.vector.tensor_copy(x_sc[:], scale_table[:].indirect(offsets[:]))
+        w1_codes, w1_scales = quantise(w1_raw, "w1")
+        halves = (slice(H, S), slice(0, H))
+        yl = []
+        for n, cols in enumerate(halves):
+            nc.vector.tensor_copy(x_codes[:, cols], word_table[:].bitcast(U32).indirect(offsets[:, cols.start // 16 : cols.stop // 16]))
+            bank = ps.tile([P, H], F32, name="yl%d" % n)
+            nc.tensor.matmul_mx(out=bank[:], lhsT=w1_codes[:].bitcast(FP8X4), lhsT_scale=w1_scales[:],
+                                rhs=x_codes[:, cols].bitcast(FP8X4), rhs_scale=x_sc[:, cols], start=True, stop=True)
+            yl.append(bank)
+        logit = sb.tile([P, S], F32, name="logit")
+        raw_ratio = sb.tile([P, S], F32, name="raw_ratio")
+        weight = sb.tile([P, S], F32, name="weight")
+        gap = sb.tile([P, S], F32, name="gap")
+        link = sb.tile([P, 2, H], F32, name="link")
+        for n, cols in enumerate(halves):
+            nc.vector.tensor_tensor(logit[:, cols], yl[n][:], mu_t[:, cols], ALU.subtract)
+        w2_codes, w2_scales = quantise(w2_raw, "w2")
+        val = ps.tile([P, S], F32, name="val")
+        nc.tensor.matmul_mx(out=val[:], lhsT=w2_codes[:].bitcast(FP8X4), lhsT_scale=w2_scales[:],
+                            rhs=x_codes[:].bitcast(FP8X4), rhs_scale=x_sc[:], start=True, stop=True)
+        for n, cols in enumerate(halves):
+            nc.scalar.activation(raw_ratio[:, cols], logit[:, cols], ACT.Exp)
+            nc.vector.tensor_tensor(ratio[:, cols], raw_ratio[:, cols], cap_t[:, cols], ALU.min)
+
+        def planes(ap):
+            return ap.rearrange("p (i s) -> p s i", s=2)
+
+        nc.vector.tensor_tensor(boot[:, : S - 1], val[:, 1:], gam_t[:, : S - 1], ALU.mult)
+        nc.vector.scalar_tensor_tensor(gap[:], val[:], -1.0, rew_t[:], ALU.mult, ALU.add)
+        nc.vector.tensor_tensor(link[:], planes(ratio[:, 1 : S + 1]), planes(gam_t[:]), ALU.mult)
+        nc.vector.tensor_tensor(td[:, :, :H], planes(boot[:]), planes(gap[:]), ALU.add)
+
+        m1 = sb.tile([P, H], F32, name="m1")
+        m2 = sb.tile([P, H], F32, name="m2")
+        m3 = sb.tile([P, H], F32, name="m3")
+        m4 = sb.tile([P, H], F32, name="m4")
+        quad_link = sb.tile([P, H], F32, name="quad_link")
+        five = sb.tile([P, 2, H], F32, name="five")
+        result = sb.tile([P, S], F32, name="result")
+        tt = nc.vector.tensor_tensor
+        nc.vector.scalar_tensor_tensor(weight[:, halves[0]], yl[0][:], -1.0, ratio[:, halves[0]], ALU.mult, ALU.mult)
+        tt(m1[:], link[:, 0, :], td[:, 1, :H], ALU.mult)
+        tt(pair_link[:, :H], link[:, 0, :], link[:, 1, :], ALU.mult)
+        tt(pair_sum[:, :H], td[:, 0, :H], m1[:], ALU.add)
+        tt(quad_link[:], pair_link[:, :H], pair_link[:, 1 : H + 1], ALU.mult)
+        tt(m2[:], pair_link[:, :H], pair_sum[:, 1 : H + 1], ALU.mult)
+        tt(m4[:], quad_link[:], td[:, 0, 2 : H + 2], ALU.mult)
+        tt(quad_sum[:, :H], pair_sum[:, :H], m2[:], ALU.add)
+        nc.vector.scalar_tensor_tensor(weight[:, halves[1]], yl[1][:], -1.0, ratio[:, halves[1]], ALU.mult, ALU.mult)
+        tt(m3[:], link[:, 1, :], quad_sum[:, 1 : H + 1], ALU.mult)
+        tt(five[:, 0, :], quad_sum[:, :H], m4[:], ALU.add)
+        for cols in halves:
+            pairs = slice(cols.start // 2, cols.stop // 2)
+            tt(five[:, 1, pairs], td[:, 1, pairs], m3[:, pairs], ALU.add)
+        for n, cols in enumerate(halves):
+            tt(result[:, cols].rearrange("p (i s) -> p i s", s=2), weight[:, cols].rearrange("p (i s) -> p i s", s=2),
+               five[:, :, cols.start // 2 : cols.stop // 2].rearrange("p s i -> p i s"), ALU.mult)
+            (nc.sync if n == 0 else nc.scalar).dma_start(out[:, cols], result[:, cols])

@@ -1,6 +1,7 @@
 from contextlib import ExitStack
 
 import concourse.mybir as mybir
+from concourse.masks import make_identity
 
 F32 = mybir.dt.float32
 BF16 = mybir.dt.bfloat16
@@ -25,45 +26,44 @@ def tile_picked_yvtrac_pol_p_kernel(tc, x_words, x_scales, w1, w2, mu, cap, rew,
         sb = ctx.enter_context(tc.tile_pool(name="sb", bufs=1))
         ps = ctx.enter_context(tc.psum_pool(name="ps", bufs=1))
 
+        ps_val = ctx.enter_context(tc.psum_pool(name="ps_val", bufs=1))
         offsets = sb.tile([P, S // 16], U16, name="offsets")
         scale_table = sb.tile([P, T], U8, name="scale_table", align_bytes=64)
         word_table = sb.tile([P, T], I32, name="word_table", align_bytes=64)
-        w1_raw = sb.tile([P, 4, M], F32, name="w1_raw")
+        w1_raw = sb.tile([P, 4, M], F32, name="w1_raw", tag="w1_raw")
         w2_raw = sb.tile([P, 4, M], F32, name="w2_raw")
         mu_t = sb.tile([P, S], F32, name="mu_t")
         cap_t = sb.tile([P, S], F32, name="cap_t")
-        rew_t = sb.tile([P, S], F32, name="rew_t")
         gam_t = sb.tile([P, S], F32, name="gam_t")
+        rows = sb.tile([P, P], F32, name="rows", tag="w1_grouped", align_bytes=64)
+        identity = sb.tile([P, P], F32, name="identity")
+        nc.vector.memset(rows[:], 0.0)
+        make_identity(nc, identity[:])
 
         nc.sync.dma_start(offsets[:], offs)
-        zero = sb.tile([P, 1], F32, name="zero")
-        nc.gpsimd.memset(scale_table[:].bitcast(I32), 0)
-        nc.gpsimd.memset(zero[:], 0.0)
         for q in range(4):
-            nc.scalar.dma_start(scale_table[32 * q : 32 * q + 4, :].bitcast(I32), x_scales[0, 4 * q : 4 * q + 4, :].bitcast(I32))
-        nc.sync.dma_start(w1_raw[:], w1.rearrange("(p j) m -> p j m", j=4))
-        nc.sync.dma_start(word_table[:], x_words[0].rearrange("p n t -> p (n t)").bitcast(I32))
+            eng = nc.sync if q < 2 else nc.scalar
+            eng.dma_start(scale_table[32 * q : 32 * q + 32, :].bitcast(I32), x_scales[0, 4 * q : 4 * q + 4, :].bitcast(I32).partition_broadcast(8))
         nc.sync.dma_start(w2_raw[:], w2.rearrange("(p j) m -> p j m", j=4))
+        nc.sync.dma_start(word_table[:], x_words[0].rearrange("p n t -> p (n t)").bitcast(I32))
+        nc.sync.dma_start(rows[0:4, :], gam.rearrange("p s -> (p s)")[S - 1 : S - 1 + 4 * P].rearrange("(b n) -> b n", n=P))
+        nc.sync.dma_start(rows[4:8, :], rew[0, :].rearrange("(b n) -> b n", n=P))
+        nc.sync.dma_start(w1_raw[:], w1.rearrange("(p j) m -> p j m", j=4))
         nc.sync.dma_start(mu_t[:], mu)
         nc.sync.dma_start(cap_t[:], cap)
         nc.sync.dma_start(gam_t[:], gam)
-        nc.sync.dma_start(rew_t[:], rew)
 
-        ratio = sb.tile([P, S + PAD], F32, name="ratio")
-        boot = sb.tile([P, S], F32, name="boot")
-        td = sb.tile([P, 2, H + PAD], F32, name="td")
-        pair_sum = sb.tile([P, H + PAD], F32, name="pair_sum")
-        pair_link = sb.tile([P, H + PAD], F32, name="pair_link")
-        quad_sum = sb.tile([P, H + PAD], F32, name="quad_sum")
-        nc.vector.memset(boot[:, S - 1 : S], 0.0)
-        nc.vector.memset(td[:, 0, H:], 0.0)
-        nc.vector.memset(pair_sum[:, H:], 0.0)
-        nc.vector.memset(pair_link[:, H:], 0.0)
-        nc.vector.memset(quad_sum[:, H:], 0.0)
-        nc.scalar.activation(ratio[:, S : S + 1], zero[:], ACT.Exp)
+        zero = sb.tile([P, 1], F32, name="zero")
+        W = H + PAD
+        work = sb.tile([P, 14, W], F32, name="work")
+        M1, PAIR_SUM, PAIR_LINK, M2, QUAD_LINK, DLT0, QUAD_SUM, DLT1, GC0, GC1, M4, M3, FIVE0, FIVE1 = range(14)
+        nc.vector.memset(zero[:], 0.0)
+        nc.vector.memset(work[:, PAIR_SUM, H:], 0.0)
+        nc.vector.memset(work[:, DLT0 : QUAD_SUM + 1, H:], 0.0)
+        nc.scalar.activation(work[:, PAIR_LINK, H : H + 1], zero[:], ACT.Exp)
 
         def quantise(w_raw, name):
-            grouped = sb.tile([P, M, 4], BF16, name=name + "_grouped", align_bytes=64)
+            grouped = sb.tile([P, M, 4], BF16, name=name + "_grouped", tag=name + "_grouped", align_bytes=64)
             codes = sb.tile([P, M], U32, name=name + "_codes", align_bytes=64)
             scales = sb.tile([P, M], U8, name=name + "_scales", align_bytes=64)
             nc.scalar.copy(grouped[:].rearrange("p (c i) t -> p c t i", i=4), w_raw[:].rearrange("p t (c i) -> p c t i", i=4))
@@ -73,61 +73,103 @@ def tile_picked_yvtrac_pol_p_kernel(tc, x_words, x_scales, w1, w2, mu, cap, rew,
         x_codes = sb.tile([P, S], U32, name="x_codes", align_bytes=64)
         x_sc = sb.tile([P, S], U8, name="x_sc", align_bytes=64)
         nc.vector.tensor_copy(x_sc[:], scale_table[:].indirect(offsets[:]))
-        w1_codes, w1_scales = quantise(w1_raw, "w1")
+        w2_codes, w2_scales = quantise(w2_raw, "w2")
+        turned = ps_val.tile([P, 2 * S], F32, name="turned", offset=0)
+        nc.tensor.transpose(turned[:, 0:P], rows[:], identity[:])
+        columns = sb.tile([P, 8], F32, name="columns")
+        nc.vector.tensor_copy(columns[:], turned[:, 0:8])
+
+        def turn(bank, column, source, start=False, stop=False):
+            nc.tensor.matmul(bank[:, column : column + P], source, identity[:], is_transpose=True, start=start, stop=stop)
+
+        td = [ps.tile([P, 3 * P], F32, name="td%d" % n) for n in range(2)]
+        turn(td[0], 2 * P, zero[:].to_broadcast([P, P]), start=True)
+
         halves = (slice(H, S), slice(0, H))
-        yl = []
+        val_t = []
         for n, cols in enumerate(halves):
             nc.vector.tensor_copy(x_codes[:, cols], word_table[:].bitcast(U32).indirect(offsets[:, cols.start // 16 : cols.stop // 16]))
+            bank = ps_val.tile([P, 2, M], F32, name="val_t%d" % n, offset=n * 4 * S)
+            for u in range(2):
+                steps = slice(cols.start + u * P, cols.start + (u + 1) * P)
+                nc.tensor.matmul_mx(out=bank[:, u, :], lhsT=x_codes[:, steps].bitcast(FP8X4), lhsT_scale=x_sc[:, steps],
+                                    rhs=w2_codes[:].bitcast(FP8X4), rhs_scale=w2_scales[:], start=True, stop=True)
+            val_t.append(bank)
+        w1_codes, w1_scales = quantise(w1_raw, "w1")
+        yl = []
+        for n, cols in enumerate(halves):
             bank = ps.tile([P, H], F32, name="yl%d" % n)
             nc.tensor.matmul_mx(out=bank[:], lhsT=w1_codes[:].bitcast(FP8X4), lhsT_scale=w1_scales[:],
                                 rhs=x_codes[:, cols].bitcast(FP8X4), rhs_scale=x_sc[:, cols], start=True, stop=True)
             yl.append(bank)
+
+        boot = sb.tile([P, 4, M], F32, name="boot", tag="w1_grouped", align_bytes=64)
+        gap = sb.tile([P, 4, M], F32, name="gap", tag="w1_raw")
+        for n, cols in enumerate(halves):
+            b = cols.start // P
+            nc.vector.tensor_tensor(boot[:, b : b + 2, :], val_t[n][:], columns[:, b : b + 2].unsqueeze(2).to_broadcast([P, 2, M]), ALU.mult)
+
         logit = sb.tile([P, S], F32, name="logit")
         raw_ratio = sb.tile([P, S], F32, name="raw_ratio")
-        weight = sb.tile([P, S], F32, name="weight")
-        gap = sb.tile([P, S], F32, name="gap")
-        link = sb.tile([P, 2, H], F32, name="link")
+        ratio = sb.tile([P, S], F32, name="ratio")
         for n, cols in enumerate(halves):
             nc.vector.tensor_tensor(logit[:, cols], yl[n][:], mu_t[:, cols], ALU.subtract)
-        w2_codes, w2_scales = quantise(w2_raw, "w2")
-        val = ps.tile([P, S], F32, name="val")
-        nc.tensor.matmul_mx(out=val[:], lhsT=w2_codes[:].bitcast(FP8X4), lhsT_scale=w2_scales[:],
-                            rhs=x_codes[:].bitcast(FP8X4), rhs_scale=x_sc[:], start=True, stop=True)
-        for n, cols in enumerate(halves):
             nc.scalar.activation(raw_ratio[:, cols], logit[:, cols], ACT.Exp)
+        for n, cols in enumerate(halves):
+            b = cols.start // P
+            for u in range(2):
+                nc.scalar.activation(gap[:, b + u, :], val_t[n][:, u, :], ACT.Identity, bias=columns[:, 4 + b + u : 5 + b + u], scale=-1.0)
+        for n, cols in enumerate(halves):
             nc.vector.tensor_tensor(ratio[:, cols], raw_ratio[:, cols], cap_t[:, cols], ALU.min)
+
+        turn(td[0], 0, boot[:, 2, :])
+        turn(td[0], P, boot[:, 3, :])
+        turn(td[1], 2 * P, boot[:, 2, :], start=True)
+        turn(td[0], 1, gap[:, 2, :])
+        turn(td[0], P + 1, gap[:, 3, :], stop=True)
+        turn(td[1], 0, boot[:, 0, :])
+        turn(td[1], P, boot[:, 1, :])
+        turn(td[1], 1, gap[:, 0, :])
+        turn(td[1], P + 1, gap[:, 1, :], stop=True)
 
         def planes(ap):
             return ap.rearrange("p (i s) -> p s i", s=2)
 
-        nc.vector.tensor_tensor(boot[:, : S - 1], val[:, 1:], gam_t[:, : S - 1], ALU.mult)
-        nc.vector.scalar_tensor_tensor(gap[:], val[:], -1.0, rew_t[:], ALU.mult, ALU.add)
-        nc.vector.tensor_tensor(link[:], planes(ratio[:, 1 : S + 1]), planes(gam_t[:]), ALU.mult)
-        nc.vector.tensor_tensor(td[:, :, :H], planes(boot[:]), planes(gap[:]), ALU.add)
-
-        m1 = sb.tile([P, H], F32, name="m1")
-        m2 = sb.tile([P, H], F32, name="m2")
-        m3 = sb.tile([P, H], F32, name="m3")
-        m4 = sb.tile([P, H], F32, name="m4")
-        quad_link = sb.tile([P, H], F32, name="quad_link")
-        five = sb.tile([P, 2, H], F32, name="five")
-        result = sb.tile([P, S], F32, name="result")
         tt = nc.vector.tensor_tensor
-        nc.vector.scalar_tensor_tensor(weight[:, halves[0]], yl[0][:], -1.0, ratio[:, halves[0]], ALU.mult, ALU.mult)
-        tt(m1[:], link[:, 0, :], td[:, 1, :H], ALU.mult)
-        tt(pair_link[:, :H], link[:, 0, :], link[:, 1, :], ALU.mult)
-        tt(pair_sum[:, :H], td[:, 0, :H], m1[:], ALU.add)
-        tt(quad_link[:], pair_link[:, :H], pair_link[:, 1 : H + 1], ALU.mult)
-        tt(m2[:], pair_link[:, :H], pair_sum[:, 1 : H + 1], ALU.mult)
-        tt(m4[:], quad_link[:], td[:, 0, 2 : H + 2], ALU.mult)
-        tt(quad_sum[:, :H], pair_sum[:, :H], m2[:], ALU.add)
-        nc.vector.scalar_tensor_tensor(weight[:, halves[1]], yl[1][:], -1.0, ratio[:, halves[1]], ALU.mult, ALU.mult)
-        tt(m3[:], link[:, 1, :], quad_sum[:, 1 : H + 1], ALU.mult)
-        tt(five[:, 0, :], quad_sum[:, :H], m4[:], ALU.add)
-        for cols in halves:
-            pairs = slice(cols.start // 2, cols.stop // 2)
-            tt(five[:, 1, pairs], td[:, 1, pairs], m3[:, pairs], ALU.add)
+        result = sb.tile([P, S], F32, name="result")
+        Q = H // 2
+        starts = [cols.start // 2 for cols in halves]
+
+        def one(a, i):
+            return work[:, a, i : i + Q]
+
+        def two(a, b, i):
+            return work[:, a : b + 1 : b - a, i : i + Q]
+
+        def twice(a, i):
+            return one(a, i).unsqueeze(1).to_broadcast([P, 2, Q])
+
+        def skewed(i):
+            first = DLT0 * W + i + 2
+            return work[:].rearrange("p a w -> p (a w)")[:, first : first + 2 * (W - 1)].rearrange("p (s w) -> p s w", s=2)[:, :, :Q]
+
         for n, cols in enumerate(halves):
-            tt(result[:, cols].rearrange("p (i s) -> p i s", s=2), weight[:, cols].rearrange("p (i s) -> p i s", s=2),
-               five[:, :, cols.start // 2 : cols.stop // 2].rearrange("p s i -> p i s"), ALU.mult)
+            tt(two(GC0, GC1, starts[n]), planes(ratio[:, cols]), planes(gam_t[:, cols]), ALU.mult)
+        for n, cols in enumerate(halves):
+            tt(two(DLT0, DLT1, starts[n]), planes(td[n][:, 1 : H + 1]), planes(ratio[:, cols]), ALU.mult)
+        for i in starts:
+            tt(two(M1, PAIR_LINK, i), two(DLT1, GC1, i), twice(GC0, i), ALU.mult)
+        for i in starts:
+            tt(one(PAIR_SUM, i), one(DLT0, i), one(M1, i), ALU.add)
+        for i in starts:
+            tt(two(M2, QUAD_LINK, i), two(PAIR_SUM, PAIR_LINK, i + 1), twice(PAIR_LINK, i), ALU.mult)
+        for i in starts:
+            tt(one(QUAD_SUM, i), one(PAIR_SUM, i), one(M2, i), ALU.add)
+        for i in starts:
+            tt(two(M4, M3, i), two(QUAD_LINK, GC1, i), skewed(i), ALU.mult)
+        for i in starts:
+            tt(two(FIVE0, FIVE1, i), two(QUAD_SUM, DLT1, i), two(M4, M3, i), ALU.add)
+        for n, cols in enumerate(halves):
+            nc.vector.scalar_tensor_tensor(result[:, cols].rearrange("p (i s) -> p i s", s=2), yl[n][:].rearrange("p (i s) -> p i s", s=2), -1.0,
+                                           two(FIVE0, FIVE1, starts[n]).rearrange("p s i -> p i s"), ALU.mult, ALU.mult)
             (nc.sync if n == 0 else nc.scalar).dma_start(out[:, cols], result[:, cols])

@@ -54,13 +54,13 @@ def tile_picked_yvtrac_pol_p_kernel(tc, x_words, x_scales, w1, w2, mu, cap, rew,
         nc.sync.dma_start(gam_t[:], gam)
 
         zero = sb.tile([P, 1], F32, name="zero")
-        W = H + PAD
-        work = sb.tile([P, 14, W], F32, name="work")
+        Q = H // 2
+        W = Q + PAD
+        work = [sb.tile([P, 14, W], F32, name="work%d" % n) for n in range(2)]
         M1, PAIR_SUM, PAIR_LINK, M2, QUAD_LINK, DLT0, QUAD_SUM, DLT1, GC0, GC1, M4, M3, FIVE0, FIVE1 = range(14)
         nc.vector.memset(zero[:], 0.0)
-        nc.vector.memset(work[:, PAIR_SUM, H:], 0.0)
-        nc.vector.memset(work[:, DLT0 : QUAD_SUM + 1, H:], 0.0)
-        nc.scalar.activation(work[:, PAIR_LINK, H : H + 1], zero[:], ACT.Exp)
+        nc.vector.memset(work[0][:, DLT0 : DLT1 + 1 : 2, Q : Q + 2], 0.0)
+        nc.scalar.activation(work[0][:, GC0 : GC1 + 1, Q : Q + 2], zero[:].unsqueeze(2).to_broadcast([P, 2, 2]), ACT.Exp)
 
         def quantise(w_raw, name):
             grouped = sb.tile([P, M, 4], BF16, name=name + "_grouped", tag=name + "_grouped", align_bytes=64)
@@ -136,40 +136,39 @@ def tile_picked_yvtrac_pol_p_kernel(tc, x_words, x_scales, w1, w2, mu, cap, rew,
             return ap.rearrange("p (i s) -> p s i", s=2)
 
         tt = nc.vector.tensor_tensor
-        result = sb.tile([P, S], F32, name="result")
-        Q = H // 2
-        starts = [cols.start // 2 for cols in halves]
+        result = [sb.tile([P, H], F32, name="result%d" % n) for n in range(2)]
 
-        def one(a, i):
-            return work[:, a, i : i + Q]
+        def one(t, a, width):
+            return t[:, a, :width]
 
-        def two(a, b, i):
-            return work[:, a : b + 1 : b - a, i : i + Q]
+        def two(t, a, b, width, first=0):
+            return t[:, a : b + 1 : b - a, first : first + width]
 
-        def twice(a, i):
-            return one(a, i).unsqueeze(1).to_broadcast([P, 2, Q])
+        def twice(t, a, width):
+            return one(t, a, width).unsqueeze(1).to_broadcast([P, 2, width])
 
-        def skewed(i):
-            first = DLT0 * W + i + 2
-            return work[:].rearrange("p a w -> p (a w)")[:, first : first + 2 * (W - 1)].rearrange("p (s w) -> p s w", s=2)[:, :, :Q]
+        def skewed(t):
+            first = DLT0 * W + 2
+            return t[:].rearrange("p a w -> p (a w)")[:, first : first + 2 * (W - 1)].rearrange("p (s w) -> p s w", s=2)[:, :, :Q]
 
+        tt(two(work[0], GC0, GC1, Q), planes(ratio[:, H:]), planes(gam_t[:, H:]), ALU.mult)
+        tt(two(work[1], GC0, GC1, Q + 2), planes(ratio[:, : H + 4]), planes(gam_t[:, : H + 4]), ALU.mult)
+        tt(two(work[0], DLT0, DLT1, Q), planes(td[0][:, 1 : H + 1]), planes(ratio[:, H:]), ALU.mult)
+        tt(two(work[1], DLT0, DLT1, 2, Q), planes(td[0][:, 1:5]), planes(ratio[:, H : H + 4]), ALU.mult)
+        tt(two(work[1], DLT0, DLT1, Q), planes(td[1][:, 1 : H + 1]), planes(ratio[:, :H]), ALU.mult)
+        for t in work:
+            tt(two(t, M1, PAIR_LINK, Q + 2), two(t, DLT1, GC1, Q + 2), twice(t, GC0, Q + 2), ALU.mult)
+        for t in work:
+            tt(one(t, PAIR_SUM, Q + 2), one(t, DLT0, Q + 2), one(t, M1, Q + 2), ALU.add)
+        for t in work:
+            tt(two(t, M2, QUAD_LINK, Q + 1), two(t, PAIR_SUM, PAIR_LINK, Q + 1, 1), twice(t, PAIR_LINK, Q + 1), ALU.mult)
+        for t in work:
+            tt(one(t, QUAD_SUM, Q + 1), one(t, PAIR_SUM, Q + 1), one(t, M2, Q + 1), ALU.add)
+        for t in work:
+            tt(two(t, M4, M3, Q), two(t, QUAD_LINK, GC1, Q), skewed(t), ALU.mult)
+        for t in work:
+            tt(two(t, FIVE0, FIVE1, Q), two(t, QUAD_SUM, DLT1, Q), two(t, M4, M3, Q), ALU.add)
         for n, cols in enumerate(halves):
-            tt(two(GC0, GC1, starts[n]), planes(ratio[:, cols]), planes(gam_t[:, cols]), ALU.mult)
-        for n, cols in enumerate(halves):
-            tt(two(DLT0, DLT1, starts[n]), planes(td[n][:, 1 : H + 1]), planes(ratio[:, cols]), ALU.mult)
-        for i in starts:
-            tt(two(M1, PAIR_LINK, i), two(DLT1, GC1, i), twice(GC0, i), ALU.mult)
-        for i in starts:
-            tt(one(PAIR_SUM, i), one(DLT0, i), one(M1, i), ALU.add)
-        for i in starts:
-            tt(two(M2, QUAD_LINK, i), two(PAIR_SUM, PAIR_LINK, i + 1), twice(PAIR_LINK, i), ALU.mult)
-        for i in starts:
-            tt(one(QUAD_SUM, i), one(PAIR_SUM, i), one(M2, i), ALU.add)
-        for i in starts:
-            tt(two(M4, M3, i), two(QUAD_LINK, GC1, i), skewed(i), ALU.mult)
-        for i in starts:
-            tt(two(FIVE0, FIVE1, i), two(QUAD_SUM, DLT1, i), two(M4, M3, i), ALU.add)
-        for n, cols in enumerate(halves):
-            nc.vector.scalar_tensor_tensor(result[:, cols].rearrange("p (i s) -> p i s", s=2), yl[n][:].rearrange("p (i s) -> p i s", s=2), -1.0,
-                                           two(FIVE0, FIVE1, starts[n]).rearrange("p s i -> p i s"), ALU.mult, ALU.mult)
-            (nc.sync if n == 0 else nc.scalar).dma_start(out[:, cols], result[:, cols])
+            nc.vector.scalar_tensor_tensor(result[n][:].rearrange("p (i s) -> p i s", s=2), yl[n][:].rearrange("p (i s) -> p i s", s=2), -1.0,
+                                           two(work[n], FIVE0, FIVE1, Q).rearrange("p s i -> p i s"), ALU.mult, ALU.mult)
+            (nc.sync if n == 0 else nc.scalar).dma_start(out[:, cols], result[n][:])

from contextlib import ExitStack

import concourse.mybir as mybir
from concourse.masks import make_identity

F32 = mybir.dt.float32
BF16 = mybir.dt.bfloat16
I32 = mybir.dt.int32
U32 = mybir.dt.uint32
U16 = mybir.dt.uint16
U8 = mybir.dt.uint8
FP8X4 = mybir.dt.float8_e4m3fn_x4
ALU = mybir.AluOpType
ACT = mybir.ActivationFunctionType

P = 128
K, T, S, M = 512, 1024, 512, 128
H = S // 2
PAD = 8
FLOPS = 2 * 2 * K * M * S


def tile_picked_yvtrac_pol_p_kernel(tc, x_words, x_scales, w1, w2, mu, cap, rew, gam, offs, out):
    nc = tc.nc
    with ExitStack() as ctx:
        sb = ctx.enter_context(tc.tile_pool(name="sb", bufs=1))
        ps = ctx.enter_context(tc.psum_pool(name="ps", bufs=1))

        ps_val = ctx.enter_context(tc.psum_pool(name="ps_val", bufs=1))
        offsets = sb.tile([P, S // 16], U16, name="offsets")
        scale_table = sb.tile([P, T], U8, name="scale_table", align_bytes=64)
        word_table = sb.tile([P, T], I32, name="word_table", align_bytes=64)
        w1_raw = sb.tile([P, 4, M], F32, name="w1_raw", tag="w1_raw")
        w2_raw = sb.tile([P, 4, M], F32, name="w2_raw")
        mu_t = sb.tile([P, S], F32, name="mu_t")
        cap_t = sb.tile([P, S], F32, name="cap_t")
        gam_t = sb.tile([P, S], F32, name="gam_t")
        rows = sb.tile([P, P], F32, name="rows", tag="w1_grouped", align_bytes=64)
        identity = sb.tile([P, P], F32, name="identity")
        nc.vector.memset(rows[:], 0.0)
        make_identity(nc, identity[:])

        nc.sync.dma_start(offsets[:], offs)
        for q in range(4):
            eng = nc.sync if q < 2 else nc.scalar
            eng.dma_start(scale_table[32 * q : 32 * q + 32, :].bitcast(I32), x_scales[0, 4 * q : 4 * q + 4, :].bitcast(I32).partition_broadcast(8))
        nc.sync.dma_start(w2_raw[:], w2.rearrange("(p j) m -> p j m", j=4))
        nc.sync.dma_start(word_table[:], x_words[0].rearrange("p n t -> p (n t)").bitcast(I32))
        nc.sync.dma_start(rows[0:4, :], gam.rearrange("p s -> (p s)")[S - 1 : S - 1 + 4 * P].rearrange("(b n) -> b n", n=P))
        nc.sync.dma_start(rows[4:8, :], rew[0, :].rearrange("(b n) -> b n", n=P))
        nc.sync.dma_start(w1_raw[:], w1.rearrange("(p j) m -> p j m", j=4))
        nc.sync.dma_start(mu_t[:], mu)
        nc.sync.dma_start(cap_t[:], cap)
        nc.sync.dma_start(gam_t[:], gam)

        zero = sb.tile([P, 1], F32, name="zero")
        Q = H // 2
        W = Q + PAD
        work = [sb.tile([P, 14, W], F32, name="work%d" % n) for n in range(2)]
        M1, PAIR_SUM, PAIR_LINK, M2, QUAD_LINK, DLT0, QUAD_SUM, DLT1, GC0, GC1, M4, M3, FIVE0, FIVE1 = range(14)
        nc.vector.memset(zero[:], 0.0)
        nc.vector.memset(work[0][:, DLT0 : DLT1 + 1 : 2, Q : Q + 2], 0.0)
        nc.scalar.activation(work[0][:, GC0 : GC1 + 1, Q : Q + 2], zero[:].unsqueeze(2).to_broadcast([P, 2, 2]), ACT.Exp)

        def quantise(w_raw, name):
            grouped = sb.tile([P, M, 4], BF16, name=name + "_grouped", tag=name + "_grouped", align_bytes=64)
            codes = sb.tile([P, M], U32, name=name + "_codes", align_bytes=64)
            scales = sb.tile([P, M], U8, name=name + "_scales", align_bytes=64)
            nc.scalar.copy(grouped[:].rearrange("p (c i) t -> p c t i", i=4), w_raw[:].rearrange("p t (c i) -> p c t i", i=4))
            nc.vector.quantize_mx(out=codes[:].bitcast(FP8X4), scales=scales[:], in_=grouped[:].rearrange("p m t -> p (m t)"))
            return codes, scales

        x_codes = sb.tile([P, S], U32, name="x_codes", align_bytes=64)
        x_sc = sb.tile([P, S], U8, name="x_sc", align_bytes=64)
        nc.vector.tensor_copy(x_sc[:], scale_table[:].indirect(offsets[:]))
        w2_codes, w2_scales = quantise(w2_raw, "w2")
        turned = ps_val.tile([P, 2 * S], F32, name="turned", offset=0)
        nc.tensor.transpose(turned[:, 0:P], rows[:], identity[:])
        columns = sb.tile([P, 8], F32, name="columns")
        nc.vector.tensor_copy(columns[:], turned[:, 0:8])

        def turn(bank, column, source, start=False, stop=False):
            nc.tensor.matmul(bank[:, column : column + P], source, identity[:], is_transpose=True, start=start, stop=stop)

        td = [ps.tile([P, 3 * P], F32, name="td%d" % n) for n in range(2)]
        turn(td[0], 2 * P, zero[:].to_broadcast([P, P]), start=True)

        halves = (slice(H, S), slice(0, H))
        val_t = []
        for n, cols in enumerate(halves):
            nc.vector.tensor_copy(x_codes[:, cols], word_table[:].bitcast(U32).indirect(offsets[:, cols.start // 16 : cols.stop // 16]))
            bank = ps_val.tile([P, 2, M], F32, name="val_t%d" % n, offset=n * 4 * S)
            for u in range(2):
                steps = slice(cols.start + u * P, cols.start + (u + 1) * P)
                nc.tensor.matmul_mx(out=bank[:, u, :], lhsT=x_codes[:, steps].bitcast(FP8X4), lhsT_scale=x_sc[:, steps],
                                    rhs=w2_codes[:].bitcast(FP8X4), rhs_scale=w2_scales[:], start=True, stop=True)
            val_t.append(bank)
        w1_codes, w1_scales = quantise(w1_raw, "w1")
        yl = []
        for n, cols in enumerate(halves):
            bank = ps.tile([P, H], F32, name="yl%d" % n)
            nc.tensor.matmul_mx(out=bank[:], lhsT=w1_codes[:].bitcast(FP8X4), lhsT_scale=w1_scales[:],
                                rhs=x_codes[:, cols].bitcast(FP8X4), rhs_scale=x_sc[:, cols], start=True, stop=True)
            yl.append(bank)

        boot = sb.tile([P, 4, M], F32, name="boot", tag="w1_grouped", align_bytes=64)
        gap = sb.tile([P, 4, M], F32, name="gap", tag="w1_raw")
        for n, cols in enumerate(halves):
            b = cols.start // P
            nc.vector.tensor_tensor(boot[:, b : b + 2, :], val_t[n][:], columns[:, b : b + 2].unsqueeze(2).to_broadcast([P, 2, M]), ALU.mult)

        logit = sb.tile([P, S], F32, name="logit")
        raw_ratio = sb.tile([P, S], F32, name="raw_ratio")
        ratio = sb.tile([P, S], F32, name="ratio")
        for n, cols in enumerate(halves):
            nc.vector.tensor_tensor(logit[:, cols], yl[n][:], mu_t[:, cols], ALU.subtract)
            nc.scalar.activation(raw_ratio[:, cols], logit[:, cols], ACT.Exp)
        for n, cols in enumerate(halves):
            b = cols.start // P
            for u in range(2):
                nc.scalar.activation(gap[:, b + u, :], val_t[n][:, u, :], ACT.Identity, bias=columns[:, 4 + b + u : 5 + b + u], scale=-1.0)
        for n, cols in enumerate(halves):
            nc.vector.tensor_tensor(ratio[:, cols], raw_ratio[:, cols], cap_t[:, cols], ALU.min)

        turn(td[0], 0, boot[:, 2, :])
        turn(td[0], P, boot[:, 3, :])
        turn(td[1], 2 * P, boot[:, 2, :], start=True)
        turn(td[0], 1, gap[:, 2, :])
        turn(td[0], P + 1, gap[:, 3, :], stop=True)
        turn(td[1], 0, boot[:, 0, :])
        turn(td[1], P, boot[:, 1, :])
        turn(td[1], 1, gap[:, 0, :])
        turn(td[1], P + 1, gap[:, 1, :], stop=True)

        def planes(ap):
            return ap.rearrange("p (i s) -> p s i", s=2)

        tt = nc.vector.tensor_tensor
        result = [sb.tile([P, H], F32, name="result%d" % n) for n in range(2)]

        def one(t, a, width):
            return t[:, a, :width]

        def two(t, a, b, width, first=0):
            return t[:, a : b + 1 : b - a, first : first + width]

        def twice(t, a, width):
            return one(t, a, width).unsqueeze(1).to_broadcast([P, 2, width])

        def skewed(t):
            first = DLT0 * W + 2
            return t[:].rearrange("p a w -> p (a w)")[:, first : first + 2 * (W - 1)].rearrange("p (s w) -> p s w", s=2)[:, :, :Q]

        tt(two(work[0], GC0, GC1, Q), planes(ratio[:, H:]), planes(gam_t[:, H:]), ALU.mult)
        tt(two(work[1], GC0, GC1, Q + 2), planes(ratio[:, : H + 4]), planes(gam_t[:, : H + 4]), ALU.mult)
        tt(two(work[0], DLT0, DLT1, Q), planes(td[0][:, 1 : H + 1]), planes(ratio[:, H:]), ALU.mult)
        tt(two(work[1], DLT0, DLT1, 2, Q), planes(td[0][:, 1:5]), planes(ratio[:, H : H + 4]), ALU.mult)
        tt(two(work[1], DLT0, DLT1, Q), planes(td[1][:, 1 : H + 1]), planes(ratio[:, :H]), ALU.mult)
        for t in work:
            tt(two(t, M1, PAIR_LINK, Q + 2), two(t, DLT1, GC1, Q + 2), twice(t, GC0, Q + 2), ALU.mult)
        for t in work:
            tt(one(t, PAIR_SUM, Q + 2), one(t, DLT0, Q + 2), one(t, M1, Q + 2), ALU.add)
        for t in work:
            tt(two(t, M2, QUAD_LINK, Q + 1), two(t, PAIR_SUM, PAIR_LINK, Q + 1, 1), twice(t, PAIR_LINK, Q + 1), ALU.mult)
        for t in work:
            tt(one(t, QUAD_SUM, Q + 1), one(t, PAIR_SUM, Q + 1), one(t, M2, Q + 1), ALU.add)
        for t in work:
            tt(two(t, M4, M3, Q), two(t, QUAD_LINK, GC1, Q), skewed(t), ALU.mult)
        for t in work:
            tt(two(t, FIVE0, FIVE1, Q), two(t, QUAD_SUM, DLT1, Q), two(t, M4, M3, Q), ALU.add)
        for n, cols in enumerate(halves):
            nc.vector.scalar_tensor_tensor(result[n][:].rearrange("p (i s) -> p i s", s=2), yl[n][:].rearrange("p (i s) -> p i s", s=2), -1.0,
                                           two(work[n], FIVE0, FIVE1, Q).rearrange("p s i -> p i s"), ALU.mult, ALU.mult)
            (nc.sync if n == 0 else nc.scalar).dma_start(out[:, cols], result[n][:])
